import numpy as np
import ml_dtypes


def mxq(x, axis, fmt="e4m3"):
    dtype, down = {"e4m3": (ml_dtypes.float8_e4m3fn, 7), "e5m2": (ml_dtypes.float8_e5m2, 14)}[fmt]
    v = np.moveaxis(np.asarray(x, np.float32).astype(ml_dtypes.bfloat16).astype(np.float64), axis, -1)
    blocks = v.reshape(v.shape[:-1] + (-1, 32))
    amax = np.abs(blocks).max(-1, keepdims=True)
    byte = np.maximum(np.where(amax > 0, np.frexp(amax)[1] - 1 + 127, 0) - down, 1)
    scale = np.exp2(byte - 127.0)
    codes = (blocks / scale).astype(np.float32).astype(dtype).astype(np.float64)
    return np.moveaxis((codes * scale).reshape(v.shape), -1, axis)


WIDE = False


def mx_kscale(k):
    if not WIDE:
        return np.ones(k)
    levels = np.array([10, -10, 5, -5, 0])
    if k % 512:
        return np.exp2(np.random.permutation(np.resize(levels, k // 32))).repeat(32)
    a = np.empty((k // 512, 16))
    for p in range(k // 512):
        a[p, :8] = np.random.permutation(np.resize(levels, 8))
        for g in range(8):
            far = levels[np.abs(levels - a[p, g]) >= 10]
            a[p, g + 8] = far[np.random.randint(len(far))]
    return np.exp2(a.ravel()).repeat(32)


BF16 = ml_dtypes.bfloat16


def bf(x):
    return np.asarray(x, np.float32).astype(BF16)


def f64(x):
    return np.asarray(x).astype(np.float64)


E2M1 = np.array([0.0, 0.5, 1.0, 1.5, 2.0, 3.0, 4.0, 6.0, -0.0, -0.5, -1.0, -1.5, -2.0, -3.0, -4.0, -6.0])


def pack_weight(w, fmt):
    k, n = w.shape
    w = f64(bf(w)).reshape(k // 32, 32, n)
    amax = np.abs(w).max(1)
    if fmt == "e4m3":
        byte = np.frexp(amax)[1] - 1 + 127 - 7
    else:
        mant, ex = np.frexp(amax / 6.0)
        byte = np.where(mant > 0.5, ex, ex - 1) + 127
    byte = np.clip(np.where(amax > 0, byte, 1), 1, 254)
    scaled = (w * np.exp2(127.0 - byte)[:, None, :]).reshape(k, n).astype(np.float32)
    by_word = np.ascontiguousarray(scaled.reshape(k // 512, 128, 4, n).transpose(0, 1, 3, 2))
    if fmt == "e4m3":
        words = by_word.astype(ml_dtypes.float8_e4m3fn).view(np.uint8)
    else:
        c = by_word.astype(ml_dtypes.float4_e2m1fn).view(np.uint8) & 0xF
        words = c[..., 0::2] | (c[..., 1::2] << 4)
    return np.ascontiguousarray(words), np.ascontiguousarray(byte.astype(np.uint8).reshape(k // 512, 16, n))


def unpack_weight(words, scales, fmt):
    g, p, n, _ = words.shape
    if fmt == "e4m3":
        vals = np.ascontiguousarray(words).view(ml_dtypes.float8_e4m3fn).astype(np.float64)
    else:
        nib = np.empty((g, p, n, 4), np.uint8)
        nib[..., 0::2] = words & 0xF
        nib[..., 1::2] = words >> 4
        vals = E2M1[nib]
    vals = vals * np.repeat(np.exp2(scales.astype(np.float64) - 127.0), 8, axis=1)[..., None]
    return vals.transpose(0, 1, 3, 2).reshape(g * 512, n)
def pack4(w):
    words, scales = pack_weight(w, "e2m1")
    return words.reshape(words.shape[0], 128, -1), scales


def unpack4(words, scales):
    return unpack_weight(words.reshape(words.shape[0], 128, -1, 2), scales, "e2m1")


def planes(Y):
    n, m = Y.shape
    b = f64(bf(Y)).reshape(n // 32, 32, m)
    amax = np.abs(b).max(1)
    byte = np.clip(np.where(amax > 0, np.frexp(amax)[1] - 1 + 127 - 7, 1), 1, 254)
    codes = (b * np.exp2(127.0 - byte)[:, None, :]).reshape(n, m).astype(np.float32).astype(ml_dtypes.float8_e4m3fn).view(np.uint8)
    words = codes.reshape(n // 512, 128, 4, m).transpose(0, 1, 3, 2)
    return np.ascontiguousarray(words), np.ascontiguousarray(byte.astype(np.uint8).reshape(n // 512, 16, m))


M, K, F, N = 1024, 2048, 1024, 1536


def setup_inputs():
    s = mx_kscale(K)
    t = mx_kscale(F)
    levels = np.random.randn(M, K)
    x_words, x_scales = pack_weight((levels * s).T, "e4m3")
    loadings = np.random.randn(K, F) / np.sqrt(K)
    l_words, l_scales = pack4(loadings * t / s[:, None])
    spread = np.exp(0.8 * np.random.randn(N))
    assoc = np.random.randn(F, N) / np.sqrt(F) * spread
    bias = 0.3 * np.random.randn(N)
    return {
        "x_words": x_words,
        "x_scales": x_scales,
        "l_words": l_words,
        "l_scales": l_scales,
        "assoc": bf(assoc / t[:, None]),
        "bias": bf(bias),
    }


def reference(x_words, x_scales, l_words, l_scales, assoc, bias):
    XT = unpack_weight(x_words, x_scales, "e4m3")
    L = unpack4(l_words, l_scales)
    H = np.abs(XT.T @ L)
    y = (mxq(H, 1, "e4m3") @ mxq(f64(assoc), 0, "e4m3")) + f64(bias)
    Y = y.T
    words, scales = planes(Y)
    return y, words, scales

@@ -1,0 +1,345 @@
+from contextlib import ExitStack
+
+import concourse.mybir as mybir
+from concourse.masks import make_identity
+
+M, K, F, N = 1024, 2048, 1024, 1536
+FLOPS = 2 * M * K * F + 2 * M * F * N
+
+F32 = mybir.dt.float32
+BF16 = mybir.dt.bfloat16
+I32 = mybir.dt.int32
+U32 = mybir.dt.uint32
+U8 = mybir.dt.uint8
+FP8X4 = mybir.dt.float8_e4m3fn_x4
+FP4X4 = mybir.dt.float4_e2m1fn_x4
+ACT = mybir.ActivationFunctionType
+ALU = mybir.AluOpType
+
+P = 128
+W = 512
+
+
+def tile_metabolite_factor_diagnosis_weights_h2_kernel(
+    tc, x_words, x_scales, l_words, l_scales, assoc, bias, out_0, out_1, out_2
+):
+    nc = tc.nc
+    with ExitStack() as ctx:
+        keep = ctx.enter_context(tc.tile_pool(name="keep", bufs=1))
+        work = ctx.enter_context(tc.tile_pool(name="work", bufs=2))
+        psum = ctx.enter_context(tc.psum_pool(name="psum", bufs=1))
+        ctx.enter_context(tc.manual_schedule())
+
+        banks_used = []
+
+        def next_bank():
+            index = len(banks_used) % 8
+            bank = psum.tile([P, W], F32, name="bank%d" % index, tag="bank%d" % index)
+            banks_used.append(bank)
+            return bank
+
+        def kept(name, shape, dtype):
+            return keep.tile(shape, dtype, name=name, tag=name, align_bytes=256)
+
+        x_code = {}
+        x_scale = [kept("x_scale%d" % h, [P, 4, W], U8) for h in range(2)]
+        l_raw = {}
+        l_scale_raw = [kept("l_scale_raw%d" % g, [P, 4, W], U8) for g in range(2)]
+        l_scale = [kept("l_scale%d" % g, [P, 4, W], U8) for g in range(2)]
+        l_code = {}
+        a_raw = {}
+        a_code = [kept("a_code%d" % g, [P, N], U32) for g in range(2)]
+        a_scale = [kept("a_scale%d" % g, [P, N], U8) for g in range(2)]
+        a_words = {}
+        h_bank = {}
+        h_abs = {}
+        h_words = {}
+        h_code = {}
+        h_scale = {}
+        y_bank = {}
+        y_f32 = {}
+        y_bf = {}
+        t_bank = {}
+        yt_words = {}
+        y_code = {}
+        y_scale = [kept("y_scale0", [P, 3, 768], U8), kept("y_scale1", [P, 3, 256], U8)]
+        identity = kept("identity", [P, P], F32)
+        bias_col = kept("bias_col", [P, 2, 6], BF16)
+        bias_row = kept("bias_row", [P, N], BF16)
+
+        def load_x(h, k0, k1):
+            t = kept("x_code%d_%d" % (h, k0), [P, k1 - k0, W], U32)
+            src = x_words[k0:k1].rearrange("k p m t -> p k (m t)")[:, :, h * 2048 : (h + 1) * 2048]
+            nc.sync.dma_start(out=t[:].bitcast(I32), in_=src.bitcast(I32))
+            x_code.update({(h, k): t[:, k - k0, :] for k in range(k0, k1)})
+
+        def load_l(g, k0, k1):
+            t = kept("l_raw%d_%d" % (g, k0), [P, k1 - k0, 256], I32)
+            src = l_words[k0:k1].rearrange("k p b -> p k b")[:, :, g * 1024 : (g + 1) * 1024]
+            nc.sync.dma_start(out=t[:], in_=src.bitcast(I32))
+            l_raw.update({(g, k): t[:, k - k0, :] for k in range(k0, k1)})
+
+        def load_scales(queue, plane, rows, half):
+            for q in range(4):
+                src = rows[:, 4 * q : 4 * q + 4, half * W : (half + 1) * W].rearrange("k r n -> r k n")
+                queue.dma_start(out=plane[32 * q : 32 * q + 4, :, :].bitcast(I32), in_=src.bitcast(I32))
+
+        def load_a(g, c0, c1):
+            t = kept("a_raw%d_%d" % (g, c0), [P, 4, (c1 - c0) * W], BF16)
+            rows = assoc[g * W : (g + 1) * W, c0 * W : c1 * W].rearrange("(q t r) n -> t q r n", t=4, r=8)
+            for slot in range(4):
+                nc.sync.dma_start(out=t[:, slot, :], in_=rows[slot])
+            a_raw.update({(g, c): t[:, :, (c - c0) * W : (c - c0 + 1) * W] for c in range(c0, c1)})
+
+        def sort_l(g, k):
+            t = kept("l_code%d_%d" % (g, k), [P, 1024], U8)
+            nc.vector.tensor_copy(
+                out=t[:].bitcast(I32).rearrange("p (t q w) -> p t q w", t=4, w=4),
+                in_=l_raw[g, k].rearrange("p (q t w) -> p t q w", t=4, w=4),
+            )
+            l_code.update({(g, k): t})
+
+        def sort_l_scales(g):
+            nc.vector.tensor_copy(
+                out=l_scale[g][:].bitcast(I32).rearrange("p k (t q w) -> p k t q w", t=4, w=2),
+                in_=l_scale_raw[g][:].bitcast(I32).rearrange("p k (q t w) -> p k t q w", t=4, w=2),
+            )
+
+        def interleave(engine, name, src):
+            t = work.tile([P, W, 4], BF16, name=name, tag=name, bufs=3, align_bytes=256)
+            dst = t[:].rearrange("p (c i) t -> p c t i", i=4)
+            view = src.rearrange("p t (c i) -> p c t i", i=4)
+            if engine == "vector":
+                nc.vector.tensor_copy(out=dst, in_=view)
+            else:
+                nc.scalar.copy(out=dst, in_=view)
+            return t
+
+        def interleave_a(engine, g, c):
+            a_words.update({(g, c): interleave(engine, "a_words", a_raw[g, c])})
+
+        def quantize_a(g, c):
+            cols = slice(c * W, (c + 1) * W)
+            nc.vector.quantize_mx(
+                out=a_code[g][:, cols].bitcast(FP8X4),
+                scales=a_scale[g][:, cols],
+                in_=a_words[g, c][:].rearrange("p n t -> p (n t)"),
+            )
+
+        def factor_pass(h, g, slot, k):
+            if k == 0:
+                h_bank.update({(h, g, slot): next_bank()})
+            nc.tensor.matmul_mx(
+                out=h_bank[h, g, slot][:],
+                lhsT=l_code[g, k][:, slot * 256 : (slot + 1) * 256].bitcast(FP4X4),
+                lhsT_scale=l_scale[g][:, k, slot * P : (slot + 1) * P],
+                rhs=x_code[h, k].bitcast(FP8X4),
+                rhs_scale=x_scale[h][:, k, :],
+                start=(k == 0),
+                stop=(k == 3),
+            )
+
+        def factor_slot(h, g, slot):
+            for k in range(4):
+                factor_pass(h, g, slot, k)
+
+        def abs_slot(h, g, slot):
+            if slot == 0:
+                h_abs.update({(h, g): work.tile([P, 4, W], BF16, name="h_abs", tag="h_abs", align_bytes=256)})
+            nc.scalar.activation(out=h_abs[h, g][:, slot, :], in_=h_bank[h, g, slot][:], func=ACT.Abs)
+
+        def interleave_h(engine, h, g):
+            h_words.update({(h, g): interleave(engine, "h_words", h_abs[h, g][:])})
+
+        def quantize_h(h, g):
+            h_code.update({(h, g): kept("h_code%d_%d" % (h, g), [P, W], U32)})
+            h_scale.update({(h, g): kept("h_scale%d_%d" % (h, g), [P, W], U8)})
+            nc.vector.quantize_mx(
+                out=h_code[h, g][:].bitcast(FP8X4),
+                scales=h_scale[h, g][:],
+                in_=h_words[h, g][:].rearrange("p m t -> p (m t)"),
+            )
+
+        def product(i, c):
+            h, j = divmod(i, 4)
+            rows = slice(j * P, (j + 1) * P)
+            cols = slice(c * W, (c + 1) * W)
+            bank = next_bank()
+            y_bank.update({(i, c): bank})
+            for g in range(2):
+                nc.tensor.matmul_mx(
+                    out=bank[:],
+                    lhsT=h_code[h, g][:, rows].bitcast(FP8X4),
+                    lhsT_scale=h_scale[h, g][:, rows],
+                    rhs=a_code[g][:, cols].bitcast(FP8X4),
+                    rhs_scale=a_scale[g][:, cols],
+                    start=(g == 0),
+                    stop=(g == 1),
+                )
+
+        def add_bias(i, c):
+            if c == 0:
+                y_f32.update({i: work.tile([P, N], F32, name="y_f32", tag="y_f32", bufs=6)})
+            cols = slice(c * W, (c + 1) * W)
+            nc.vector.tensor_tensor(out=y_f32[i][:, cols], in0=y_bank[i, c][:], in1=bias_row[:, cols], op=ALU.add)
+
+        def round_y(engine, i, c):
+            if c == 0:
+                y_bf.update({i: work.tile([P, N], BF16, name="y_bf", tag="y_bf", bufs=4, align_bytes=256)})
+            cols = slice(c * W, (c + 1) * W)
+            dst = y_bf[i][:, cols].rearrange("m (u p e) -> m u p e", u=2, e=2)
+            src = y_f32[i][:, cols].rearrange("m (p u e) -> m u p e", u=2, e=2)
+            if engine == "vector":
+                nc.vector.tensor_copy(out=dst, in_=src)
+            else:
+                nc.scalar.copy(out=dst, in_=src)
+
+        def store_y(i):
+            nc.sync.dma_start(out=out_0[i * P : (i + 1) * P, :], in_=y_f32[i][:])
+
+        def turn(pair, g):
+            bank = next_bank()
+            t_bank.update({(pair, g): bank})
+            for j in range(2):
+                words = y_bf[2 * pair + j][:].bitcast(F32)
+                for u in range(2):
+                    nc.tensor.transpose(
+                        bank[:, u * 256 + j * P : u * 256 + (j + 1) * P],
+                        words[:, g * 256 + u * P : g * 256 + (u + 1) * P],
+                        identity[:],
+                    )
+
+        def gather_words(pair, g):
+            t = work.tile([P, 1024], BF16, name="yt_words", tag="yt_words", bufs=3, align_bytes=256)
+            nc.scalar.copy(
+                out=t[:].bitcast(F32).rearrange("p (m u) -> p m u", u=2),
+                in_=t_bank[pair, g][:].rearrange("p (u m) -> p m u", u=2),
+            )
+            yt_words.update({(pair, g): t})
+
+        def quantize_y(pair, g):
+            if g == 0:
+                y_code.update({pair: kept("y_code%d" % pair, [P, 3, 256], U32)})
+            plane = y_scale[0][:, g, pair * 256 : (pair + 1) * 256] if pair < 3 else y_scale[1][:, g, :]
+            nc.vector.quantize_mx(out=y_code[pair][:, g, :].bitcast(FP8X4), scales=plane, in_=yt_words[pair, g][:])
+
+        def store_codes(pair):
+            dst = out_1.rearrange("g p m t -> p g (m t)")[:, :, pair * 1024 : (pair + 1) * 1024]
+            nc.sync.dma_start(out=dst.bitcast(I32), in_=y_code[pair][:].bitcast(I32))
+
+        def store_scales(part, m0, m1):
+            for q in range(4):
+                dst = out_2[:, 4 * q : 4 * q + 4, m0:m1].rearrange("g r m -> r g m")
+                nc.sync.dma_start(out=dst.bitcast(I32), in_=y_scale[part][32 * q : 32 * q + 4, :, :].bitcast(I32))
+
+        def tile_product(i, vector_rounds=()):
+            for c in range(3):
+                product(i, c)
+                add_bias(i, c)
+                round_y("vector" if c in vector_rounds else "scalar", i, c)
+            store_y(i)
+
+        def planes(pair):
+            for g in range(3):
+                turn(pair, g)
+                gather_words(pair, g)
+
+        def finish(pair):
+            for g in range(3):
+                quantize_y(pair, g)
+            store_codes(pair)
+
+        nc.gpsimd.dma_start(out=bias_col[:], in_=bias.rearrange("(h p c) -> p h c", h=2, c=6))
+        load_l(0, 0, 2)
+        load_x(0, 0, 1)
+        for plane in (l_scale_raw[0], x_scale[0], l_scale_raw[1], x_scale[1]):
+            nc.vector.memset(plane[:].bitcast(I32), 0)
+        make_identity(nc, identity[:])
+        load_scales(nc.sync, l_scale_raw[0], l_scales, 0)
+        load_scales(nc.sync, x_scale[0], x_scales, 0)
+        load_scales(nc.gpsimd, l_scale_raw[1], l_scales, 1)
+        load_scales(nc.gpsimd, x_scale[1], x_scales, 1)
+        load_x(0, 1, 2)
+        load_l(0, 2, 4)
+        load_x(0, 2, 4)
+        load_a(0, 0, 1)
+        load_l(1, 0, 4)
+        load_a(1, 0, 1)
+        load_a(0, 1, 3)
+        load_x(1, 0, 2)
+        load_x(1, 2, 4)
+        load_a(1, 1, 3)
+
+        for half in range(2):
+            bank = next_bank()
+            words = bias_col[:, half, :].bitcast(F32)
+            for c in range(3):
+                nc.tensor.transpose(bank[:, c * P : (c + 1) * P], words[:, c : c + 1].to_broadcast([P, P]), identity[:])
+            nc.scalar.activation(
+                out=bias_row[:, half * 768 : (half + 1) * 768].rearrange("p (n c e) -> p n c e", c=3, e=2),
+                in_=bank[:, 0 : 3 * P].bitcast(BF16).rearrange("p (c n e) -> p n c e", c=3, e=2),
+                func=ACT.Copy,
+            )
+
+        sort_l(0, 0)
+        sort_l_scales(0)
+        for k in range(1, 4):
+            sort_l(0, k)
+        for k in range(4):
+            for slot in range(4):
+                factor_pass(0, 0, slot, k)
+        interleave_a("scalar", 0, 0)
+        sort_l_scales(1)
+        for k in range(4):
+            sort_l(1, k)
+        for slot in range(4):
+            abs_slot(0, 0, slot)
+        interleave_a("vector", 1, 0)
+        quantize_a(0, 0)
+        for slot in range(4):
+            factor_slot(0, 1, slot)
+            abs_slot(0, 1, slot)
+        interleave_h("vector", 0, 0)
+        quantize_a(1, 0)
+        interleave_a("vector", 0, 2)
+        quantize_h(0, 0)
+        interleave_a("scalar", 0, 1)
+        interleave_h("vector", 0, 1)
+        quantize_a(0, 2)
+        for slot in range(4):
+            factor_slot(1, 0, slot)
+            abs_slot(1, 0, slot)
+        interleave_a("vector", 1, 1)
+        quantize_h(0, 1)
+        quantize_a(0, 1)
+        interleave_a("vector", 1, 2)
+        quantize_a(1, 1)
+        for slot in range(2):
+            factor_slot(1, 1, slot)
+            abs_slot(1, 1, slot)
+        interleave_h("scalar", 1, 0)
+        quantize_a(1, 2)
+        tile_product(0)
+        for slot in range(2, 4):
+            factor_slot(1, 1, slot)
+            abs_slot(1, 1, slot)
+        quantize_h(1, 0)
+        tile_product(1)
+        interleave_h("vector", 1, 1)
+        tile_product(2)
+        quantize_h(1, 1)
+        planes(0)
+        tile_product(3)
+        finish(0)
+        tile_product(4, (2,))
+        planes(1)
+        tile_product(5)
+        finish(1)
+        tile_product(6, (2,))
+        planes(2)
+        tile_product(7, (2,))
+        finish(2)
+        store_scales(0, 0, 768)
+        planes(3)
+        finish(3)
+        store_scales(1, 768, 1024)

@@ -62,7 +62,7 @@ def tile_metabolite_factor_diagnosis_weights_h2_kernel(
         t_bank = {}
         yt_words = {}
         y_code = {}
-        y_scale = [kept("y_scale0", [P, 3, 768], U8), kept("y_scale1", [P, 3, 256], U8)]
+        y_scale = [kept("y_scale%d" % h, [P, 3, W], U8) for h in range(2)]
         identity = kept("identity", [P, P], F32)
         bias_col = kept("bias_col", [P, 2, 6], BF16)
         bias_row = kept("bias_row", [P, N], BF16)
@@ -105,18 +105,19 @@ def tile_metabolite_factor_diagnosis_weights_h2_kernel(
                 in_=l_scale_raw[g][:].bitcast(I32).rearrange("p k (q t w) -> p k t q w", t=4, w=2),
             )
 
-        def interleave(engine, name, src):
-            t = work.tile([P, W, 4], BF16, name=name, tag=name, bufs=3, align_bytes=256)
-            dst = t[:].rearrange("p (c i) t -> p c t i", i=4)
-            view = src.rearrange("p t (c i) -> p c t i", i=4)
+        def interleave(engine, store, key, name, src, part, parts):
+            if key not in store:
+                store.update({key: work.tile([P, W, 4], BF16, name=name, tag=name, bufs=3, align_bytes=256)})
+            cols = slice(part * W // parts, (part + 1) * W // parts)
+            dst = store[key][:, cols, :].rearrange("p (c i) t -> p c t i", i=4)
+            view = src[:, :, cols].rearrange("p t (c i) -> p c t i", i=4)
             if engine == "vector":
                 nc.vector.tensor_copy(out=dst, in_=view)
             else:
                 nc.scalar.copy(out=dst, in_=view)
-            return t
 
-        def interleave_a(engine, g, c):
-            a_words.update({(g, c): interleave(engine, "a_words", a_raw[g, c])})
+        def interleave_a(engine, g, c, part=0, parts=1):
+            interleave(engine, a_words, (g, c), "a_words", a_raw[g, c], part, parts)
 
         def quantize_a(g, c):
             cols = slice(c * W, (c + 1) * W)
@@ -148,8 +149,8 @@ def tile_metabolite_factor_diagnosis_weights_h2_kernel(
                 h_abs.update({(h, g): work.tile([P, 4, W], BF16, name="h_abs", tag="h_abs", align_bytes=256)})
             nc.scalar.activation(out=h_abs[h, g][:, slot, :], in_=h_bank[h, g, slot][:], func=ACT.Abs)
 
-        def interleave_h(engine, h, g):
-            h_words.update({(h, g): interleave(engine, "h_words", h_abs[h, g][:])})
+        def interleave_h(engine, h, g, part=0, parts=1):
+            interleave(engine, h_words, (h, g), "h_words", h_abs[h, g][:], part, parts)
 
         def quantize_h(h, g):
             h_code.update({(h, g): kept("h_code%d_%d" % (h, g), [P, W], U32)})
@@ -184,103 +185,122 @@ def tile_metabolite_factor_diagnosis_weights_h2_kernel(
             nc.vector.tensor_tensor(out=y_f32[i][:, cols], in0=y_bank[i, c][:], in1=bias_row[:, cols], op=ALU.add)
 
         def round_y(engine, i, c):
-            if c == 0:
+            if i not in y_bf:
                 y_bf.update({i: work.tile([P, N], BF16, name="y_bf", tag="y_bf", bufs=4, align_bytes=256)})
             cols = slice(c * W, (c + 1) * W)
             dst = y_bf[i][:, cols].rearrange("m (u p e) -> m u p e", u=2, e=2)
             src = y_f32[i][:, cols].rearrange("m (p u e) -> m u p e", u=2, e=2)
             if engine == "vector":
                 nc.vector.tensor_copy(out=dst, in_=src)
+            elif engine == "gpsimd":
+                nc.gpsimd.tensor_scalar(out=dst, in0=src, scalar1=1.0, scalar2=0.0, op0=ALU.mult, op1=ALU.add)
             else:
                 nc.scalar.copy(out=dst, in_=src)
 
-        def store_y(i):
-            nc.sync.dma_start(out=out_0[i * P : (i + 1) * P, :], in_=y_f32[i][:])
+        def store_y(i, c0=0, c1=3):
+            nc.sync.dma_start(out=out_0[i * P : (i + 1) * P, c0 * W : c1 * W], in_=y_f32[i][:, c0 * W : c1 * W])
 
-        def turn(pair, g):
+        def turn(tiles, g):
             bank = next_bank()
-            t_bank.update({(pair, g): bank})
-            for j in range(2):
-                words = y_bf[2 * pair + j][:].bitcast(F32)
+            t_bank.update({(tiles, g): bank})
+            width = len(tiles) * P
+            for j, i in enumerate(tiles):
+                words = y_bf[i][:].bitcast(F32)
                 for u in range(2):
                     nc.tensor.transpose(
-                        bank[:, u * 256 + j * P : u * 256 + (j + 1) * P],
+                        bank[:, u * width + j * P : u * width + (j + 1) * P],
                         words[:, g * 256 + u * P : g * 256 + (u + 1) * P],
                         identity[:],
                     )
 
-        def gather_words(pair, g):
-            t = work.tile([P, 1024], BF16, name="yt_words", tag="yt_words", bufs=3, align_bytes=256)
-            nc.scalar.copy(
-                out=t[:].bitcast(F32).rearrange("p (m u) -> p m u", u=2),
-                in_=t_bank[pair, g][:].rearrange("p (u m) -> p m u", u=2),
-            )
-            yt_words.update({(pair, g): t})
+        def gather_words(engine, tiles, g):
+            width = len(tiles) * P
+            t = work.tile([P, 4 * width], BF16, name="yt_words", tag="yt_words", bufs=6, align_bytes=256)
+            dst = t[:].bitcast(F32).rearrange("p (m u) -> p m u", u=2)
+            src = t_bank[tiles, g][:, 0 : 2 * width].rearrange("p (u m) -> p m u", u=2)
+            if engine == "vector":
+                nc.vector.tensor_copy(out=dst, in_=src)
+            else:
+                nc.scalar.copy(out=dst, in_=src)
+            yt_words.update({(tiles, g): t})
 
-        def quantize_y(pair, g):
+        def quantize_y(tiles, g):
+            width = len(tiles) * P
             if g == 0:
-                y_code.update({pair: kept("y_code%d" % pair, [P, 3, 256], U32)})
-            plane = y_scale[0][:, g, pair * 256 : (pair + 1) * 256] if pair < 3 else y_scale[1][:, g, :]
-            nc.vector.quantize_mx(out=y_code[pair][:, g, :].bitcast(FP8X4), scales=plane, in_=yt_words[pair, g][:])
+                y_code.update({tiles: kept("y_code%d" % tiles[0], [P, 3, width], U32)})
+            half, first = divmod(tiles[0] * P, W)
+            nc.vector.quantize_mx(
+                out=y_code[tiles][:, g, :].bitcast(FP8X4),
+                scales=y_scale[half][:, g, first : first + width],
+                in_=yt_words[tiles, g][:],
+            )
 
-        def store_codes(pair):
-            dst = out_1.rearrange("g p m t -> p g (m t)")[:, :, pair * 1024 : (pair + 1) * 1024]
-            nc.sync.dma_start(out=dst.bitcast(I32), in_=y_code[pair][:].bitcast(I32))
+        def store_codes(tiles, queue=nc.sync):
+            dst = out_1.rearrange("g p m t -> p g (m t)")[:, :, tiles[0] * W : (tiles[-1] + 1) * W]
+            queue.dma_start(out=dst.bitcast(I32), in_=y_code[tiles][:].bitcast(I32))
 
-        def store_scales(part, m0, m1):
-            for q in range(4):
-                dst = out_2[:, 4 * q : 4 * q + 4, m0:m1].rearrange("g r m -> r g m")
-                nc.sync.dma_start(out=dst.bitcast(I32), in_=y_scale[part][32 * q : 32 * q + 4, :, :].bitcast(I32))
+        def store_scales(half, q, queue=nc.sync):
+            dst = out_2[:, 4 * q : 4 * q + 4, half * W : (half + 1) * W].rearrange("g r m -> r g m")
+            queue.dma_start(out=dst.bitcast(I32), in_=y_scale[half][32 * q : 32 * q + 4, :, :].bitcast(I32))
 
-        def tile_product(i, vector_rounds=()):
+        def spread_bias():
+            for half in range(2):
+                bank = next_bank()
+                words = bias_col[:, half, :].bitcast(F32)
+                for c in range(3):
+                    nc.tensor.transpose(
+                        bank[:, c * P : (c + 1) * P], words[:, c : c + 1].to_broadcast([P, P]), identity[:]
+                    )
+                nc.scalar.activation(
+                    out=bias_row[:, half * 768 : (half + 1) * 768].rearrange("p (n c e) -> p n c e", c=3, e=2),
+                    in_=bank[:, 0 : 3 * P].bitcast(BF16).rearrange("p (c n e) -> p n c e", c=3, e=2),
+                    func=ACT.Copy,
+                )
+
+
+        def tile_product(i, gpsimd_rounds=(0, 1)):
             for c in range(3):
                 product(i, c)
                 add_bias(i, c)
-                round_y("vector" if c in vector_rounds else "scalar", i, c)
+                if c in gpsimd_rounds:
+                    round_y("gpsimd", i, c)
             store_y(i)
 
-        def planes(pair):
+        def planes(tiles):
             for g in range(3):
-                turn(pair, g)
-                gather_words(pair, g)
+                turn(tiles, g)
+                gather_words("scalar", tiles, g)
 
-        def finish(pair):
+        def finish(tiles):
             for g in range(3):
-                quantize_y(pair, g)
-            store_codes(pair)
+                quantize_y(tiles, g)
+            store_codes(tiles)
 
         nc.gpsimd.dma_start(out=bias_col[:], in_=bias.rearrange("(h p c) -> p h c", h=2, c=6))
-        load_l(0, 0, 2)
+        load_l(0, 0, 1)
         load_x(0, 0, 1)
         for plane in (l_scale_raw[0], x_scale[0], l_scale_raw[1], x_scale[1]):
             nc.vector.memset(plane[:].bitcast(I32), 0)
         make_identity(nc, identity[:])
         load_scales(nc.sync, l_scale_raw[0], l_scales, 0)
         load_scales(nc.sync, x_scale[0], x_scales, 0)
-        load_scales(nc.gpsimd, l_scale_raw[1], l_scales, 1)
-        load_scales(nc.gpsimd, x_scale[1], x_scales, 1)
         load_x(0, 1, 2)
-        load_l(0, 2, 4)
-        load_x(0, 2, 4)
+        load_l(0, 1, 4)
         load_a(0, 0, 1)
+        load_x(0, 2, 3)
+        load_x(0, 3, 4)
+        load_scales(nc.sync, l_scale_raw[1], l_scales, 1)
         load_l(1, 0, 4)
         load_a(1, 0, 1)
-        load_a(0, 1, 3)
+        load_a(0, 1, 2)
+        load_scales(nc.sync, x_scale[1], x_scales, 1)
         load_x(1, 0, 2)
         load_x(1, 2, 4)
-        load_a(1, 1, 3)
+        load_a(1, 1, 2)
+        load_a(0, 2, 3)
+        load_a(1, 2, 3)
 
-        for half in range(2):
-            bank = next_bank()
-            words = bias_col[:, half, :].bitcast(F32)
-            for c in range(3):
-                nc.tensor.transpose(bank[:, c * P : (c + 1) * P], words[:, c : c + 1].to_broadcast([P, P]), identity[:])
-            nc.scalar.activation(
-                out=bias_row[:, half * 768 : (half + 1) * 768].rearrange("p (n c e) -> p n c e", c=3, e=2),
-                in_=bank[:, 0 : 3 * P].bitcast(BF16).rearrange("p (c n e) -> p n c e", c=3, e=2),
-                func=ACT.Copy,
-            )
-
+        spread_bias()
         sort_l(0, 0)
         sort_l_scales(0)
         for k in range(1, 4):
@@ -288,58 +308,85 @@ def tile_metabolite_factor_diagnosis_weights_h2_kernel(
         for k in range(4):
             for slot in range(4):
                 factor_pass(0, 0, slot, k)
-        interleave_a("scalar", 0, 0)
+        interleave_a("vector", 0, 0)
+        quantize_a(0, 0)
         sort_l_scales(1)
         for k in range(4):
             sort_l(1, k)
+        interleave_a("vector", 1, 0)
         for slot in range(4):
             abs_slot(0, 0, slot)
-        interleave_a("vector", 1, 0)
-        quantize_a(0, 0)
+        interleave_h("vector", 0, 0)
+        quantize_a(1, 0)
+        quantize_h(0, 0)
         for slot in range(4):
             factor_slot(0, 1, slot)
             abs_slot(0, 1, slot)
-        interleave_h("vector", 0, 0)
-        quantize_a(1, 0)
-        interleave_a("vector", 0, 2)
-        quantize_h(0, 0)
-        interleave_a("scalar", 0, 1)
+            if slot % 2:
+                interleave_a("scalar", 0, 1, slot // 2, 2)
+        interleave_a("vector", 1, 1)
         interleave_h("vector", 0, 1)
-        quantize_a(0, 2)
+        quantize_a(0, 1)
+        quantize_a(1, 1)
+        quantize_h(0, 1)
+        interleave_a("scalar", 0, 2)
         for slot in range(4):
             factor_slot(1, 0, slot)
             abs_slot(1, 0, slot)
-        interleave_a("vector", 1, 1)
-        quantize_h(0, 1)
-        quantize_a(0, 1)
         interleave_a("vector", 1, 2)
-        quantize_a(1, 1)
+        quantize_a(0, 2)
+        quantize_a(1, 2)
+        interleave_h("scalar", 1, 0)
         for slot in range(2):
             factor_slot(1, 1, slot)
             abs_slot(1, 1, slot)
-        interleave_h("scalar", 1, 0)
-        quantize_a(1, 2)
-        tile_product(0)
+        tile_product(0, (0, 1, 2))
         for slot in range(2, 4):
             factor_slot(1, 1, slot)
             abs_slot(1, 1, slot)
         quantize_h(1, 0)
-        tile_product(1)
-        interleave_h("vector", 1, 1)
-        tile_product(2)
+        interleave_h("scalar", 1, 1)
+        tile_product(1, (0, 1, 2))
+        tile_product(2, (0,))
         quantize_h(1, 1)
-        planes(0)
-        tile_product(3)
-        finish(0)
-        tile_product(4, (2,))
-        planes(1)
-        tile_product(5)
-        finish(1)
-        tile_product(6, (2,))
-        planes(2)
-        tile_product(7, (2,))
-        finish(2)
-        store_scales(0, 0, 768)
-        planes(3)
-        finish(3)
-        store_scales(1, 768, 1024)
+        planes((0, 1))
+        round_y("scalar", 2, 1)
+        round_y("scalar", 2, 2)
+        tile_product(3, (0,))
+        round_y("scalar", 3, 1)
+        round_y("scalar", 3, 2)
+        finish((0, 1))
+        tile_product(4, (0,))
+        planes((2, 3))
+        round_y("scalar", 4, 1)
+        round_y("scalar", 4, 2)
+        tile_product(5, (0,))
+        round_y("scalar", 5, 1)
+        round_y("scalar", 5, 2)
+        finish((2, 3))
+        for q in range(4):
+            store_scales(0, q)
+        tile_product(6)
+        planes((4, 5))
+        round_y("scalar", 6, 2)
+        for c in range(3):
+            product(7, c)
+            add_bias(7, c)
+            store_y(7, c, c + 1)
+        round_y("gpsimd", 7, 0)
+        round_y("scalar", 7, 1)
+        planes((6,))
+        quantize_y((4, 5), 0)
+        round_y("vector", 7, 2)
+        quantize_y((4, 5), 1)
+        quantize_y((4, 5), 2)
+        store_codes((4, 5))
+        for g in range(3):
+            turn((7,), g)
+        finish((6,))
+        gather_words("scalar", (7,), 0)
+        gather_words("scalar", (7,), 1)
+        gather_words("vector", (7,), 2)
+        finish((7,))
+        for q in range(4):
+            store_scales(1, q, nc.scalar if q % 2 else nc.sync)

@@ -61,7 +61,7 @@ def tile_metabolite_factor_diagnosis_weights_h2_kernel(
         y_bf = {}
         t_bank = {}
         yt_words = {}
-        y_code = {}
+        y_code = [kept("y_code%d" % h, [P, 3, W], U32) for h in range(2)]
         y_scale = [kept("y_scale%d" % h, [P, 3, W], U8) for h in range(2)]
         identity = kept("identity", [P, P], F32)
         bias_col = kept("bias_col", [P, 2, 6], BF16)
@@ -73,14 +73,13 @@ def tile_metabolite_factor_diagnosis_weights_h2_kernel(
             nc.sync.dma_start(out=t[:].bitcast(I32), in_=src.bitcast(I32))
             x_code.update({(h, k): t[:, k - k0, :] for k in range(k0, k1)})
 
-        def load_l(g, k0, k1):
-            t = kept("l_raw%d_%d" % (g, k0), [P, k1 - k0, 256], I32)
-            src = l_words[k0:k1].rearrange("k p b -> p k b")[:, :, g * 1024 : (g + 1) * 1024]
-            nc.sync.dma_start(out=t[:], in_=src.bitcast(I32))
-            l_raw.update({(g, k): t[:, k - k0, :] for k in range(k0, k1)})
+        def load_l(k0, k1):
+            t = kept("l_raw%d" % k0, [P, k1 - k0, 512], I32)
+            nc.sync.dma_start(out=t[:], in_=l_words[k0:k1].rearrange("k p b -> p k b").bitcast(I32))
+            l_raw.update({(g, k): t[:, k - k0, g * 256 : (g + 1) * 256] for k in range(k0, k1) for g in range(2)})
 
-        def load_scales(queue, plane, rows, half):
-            for q in range(4):
+        def load_scales(queue, plane, rows, half, quadrants=(0, 2, 1, 3)):
+            for q in quadrants:
                 src = rows[:, 4 * q : 4 * q + 4, half * W : (half + 1) * W].rearrange("k r n -> r k n")
                 queue.dma_start(out=plane[32 * q : 32 * q + 4, :, :].bitcast(I32), in_=src.bitcast(I32))
 
@@ -226,18 +225,17 @@ def tile_metabolite_factor_diagnosis_weights_h2_kernel(
 
         def quantize_y(tiles, g):
             width = len(tiles) * P
-            if g == 0:
-                y_code.update({tiles: kept("y_code%d" % tiles[0], [P, 3, width], U32)})
             half, first = divmod(tiles[0] * P, W)
             nc.vector.quantize_mx(
-                out=y_code[tiles][:, g, :].bitcast(FP8X4),
+                out=y_code[half][:, g, first : first + width].bitcast(FP8X4),
                 scales=y_scale[half][:, g, first : first + width],
                 in_=yt_words[tiles, g][:],
             )
 
         def store_codes(tiles, queue=nc.sync):
             dst = out_1.rearrange("g p m t -> p g (m t)")[:, :, tiles[0] * W : (tiles[-1] + 1) * W]
-            queue.dma_start(out=dst.bitcast(I32), in_=y_code[tiles][:].bitcast(I32))
+            half, first = divmod(tiles[0] * P, W)
+            queue.dma_start(out=dst.bitcast(I32), in_=y_code[half][:, :, first : first + len(tiles) * P].bitcast(I32))
 
         def store_scales(half, q, queue=nc.sync):
             dst = out_2[:, 4 * q : 4 * q + 4, half * W : (half + 1) * W].rearrange("g r m -> r g m")
@@ -258,13 +256,16 @@ def tile_metabolite_factor_diagnosis_weights_h2_kernel(
                 )
 
 
-        def tile_product(i, gpsimd_rounds=(0, 1)):
+        def tile_product(i, gpsimd_rounds=(0, 1), by_chunk=False):
             for c in range(3):
                 product(i, c)
                 add_bias(i, c)
+                if by_chunk:
+                    store_y(i, c, c + 1)
                 if c in gpsimd_rounds:
                     round_y("gpsimd", i, c)
-            store_y(i)
+            if not by_chunk:
+                store_y(i)
 
         def planes(tiles):
             for g in range(3):
@@ -277,90 +278,100 @@ def tile_metabolite_factor_diagnosis_weights_h2_kernel(
             store_codes(tiles)
 
         nc.gpsimd.dma_start(out=bias_col[:], in_=bias.rearrange("(h p c) -> p h c", h=2, c=6))
-        load_l(0, 0, 1)
-        load_x(0, 0, 1)
         for plane in (l_scale_raw[0], x_scale[0], l_scale_raw[1], x_scale[1]):
             nc.vector.memset(plane[:].bitcast(I32), 0)
         make_identity(nc, identity[:])
+        load_l(0, 1)
+        load_x(0, 0, 1)
         load_scales(nc.sync, l_scale_raw[0], l_scales, 0)
         load_scales(nc.sync, x_scale[0], x_scales, 0)
         load_x(0, 1, 2)
-        load_l(0, 1, 4)
-        load_a(0, 0, 1)
-        load_x(0, 2, 3)
-        load_x(0, 3, 4)
+        load_l(1, 2)
         load_scales(nc.sync, l_scale_raw[1], l_scales, 1)
-        load_l(1, 0, 4)
-        load_a(1, 0, 1)
-        load_a(0, 1, 2)
+        load_a(0, 0, 1)
+        load_x(0, 2, 4)
+        load_l(2, 4)
+        load_a(1, 0, 2)
         load_scales(nc.sync, x_scale[1], x_scales, 1)
         load_x(1, 0, 2)
         load_x(1, 2, 4)
-        load_a(1, 1, 2)
-        load_a(0, 2, 3)
+        load_a(0, 1, 3)
         load_a(1, 2, 3)
 
         spread_bias()
         sort_l(0, 0)
+        sort_l(1, 0)
         sort_l_scales(0)
-        for k in range(1, 4):
-            sort_l(0, k)
-        for k in range(4):
-            for slot in range(4):
-                factor_pass(0, 0, slot, k)
-        interleave_a("vector", 0, 0)
-        quantize_a(0, 0)
+        sort_l(0, 1)
         sort_l_scales(1)
-        for k in range(4):
-            sort_l(1, k)
+        sort_l(1, 1)
+        for g, k in ((0, 0), (0, 1), (1, 0), (1, 1)):
+            for slot in range(4):
+                factor_pass(0, g, slot, k)
+        interleave_a("vector", 0, 0)
+        for g in range(2):
+            sort_l(g, 2)
+            sort_l(g, 3)
+        quantize_a(0, 0)
+        for g in range(2):
+            for slot in range(4):
+                factor_pass(0, g, slot, 2)
+                factor_pass(0, g, slot, 3)
+                abs_slot(0, g, slot)
         interleave_a("vector", 1, 0)
-        for slot in range(4):
-            abs_slot(0, 0, slot)
         interleave_h("vector", 0, 0)
         quantize_a(1, 0)
         quantize_h(0, 0)
-        for slot in range(4):
-            factor_slot(0, 1, slot)
-            abs_slot(0, 1, slot)
-            if slot % 2:
-                interleave_a("scalar", 0, 1, slot // 2, 2)
-        interleave_a("vector", 1, 1)
+        interleave_a("scalar", 1, 1)
         interleave_h("vector", 0, 1)
-        quantize_a(0, 1)
-        quantize_a(1, 1)
+        interleave_a("vector", 0, 1)
         quantize_h(0, 1)
+        quantize_a(1, 1)
+        quantize_a(0, 1)
         interleave_a("scalar", 0, 2)
-        for slot in range(4):
-            factor_slot(1, 0, slot)
-            abs_slot(1, 0, slot)
         interleave_a("vector", 1, 2)
+        for k in range(2):
+            for slot in range(4):
+                factor_pass(1, 0, slot, k)
+        for slot in range(4):
+            factor_pass(1, 0, slot, 2)
+            factor_pass(1, 0, slot, 3)
+            abs_slot(1, 0, slot)
         quantize_a(0, 2)
         quantize_a(1, 2)
-        interleave_h("scalar", 1, 0)
         for slot in range(2):
             factor_slot(1, 1, slot)
             abs_slot(1, 1, slot)
-        tile_product(0, (0, 1, 2))
+        for c in range(2):
+            product(0, c)
+            add_bias(0, c)
+        interleave_h("vector", 1, 0)
         for slot in range(2, 4):
             factor_slot(1, 1, slot)
             abs_slot(1, 1, slot)
+            round_y("scalar", 0, slot - 2)
+        product(0, 2)
+        add_bias(0, 2)
+        store_y(0)
         quantize_h(1, 0)
         interleave_h("scalar", 1, 1)
-        tile_product(1, (0, 1, 2))
+        round_y("gpsimd", 0, 2)
+        tile_product(1, (0, 1))
+        round_y("scalar", 1, 2)
         tile_product(2, (0,))
         quantize_h(1, 1)
         planes((0, 1))
         round_y("scalar", 2, 1)
         round_y("scalar", 2, 2)
-        tile_product(3, (0,))
+        tile_product(3, (0,), True)
         round_y("scalar", 3, 1)
         round_y("scalar", 3, 2)
         finish((0, 1))
-        tile_product(4, (0,))
+        tile_product(4, (0,), True)
         planes((2, 3))
         round_y("scalar", 4, 1)
         round_y("scalar", 4, 2)
-        tile_product(5, (0,))
+        tile_product(5, (0,), True)
         round_y("scalar", 5, 1)
         round_y("scalar", 5, 2)
         finish((2, 3))
@@ -372,7 +383,8 @@ def tile_metabolite_factor_diagnosis_weights_h2_kernel(
         for c in range(3):
             product(7, c)
             add_bias(7, c)
-            store_y(7, c, c + 1)
+            if c:
+                store_y(7, 2 * c - 2, c + 1)
         round_y("gpsimd", 7, 0)
         round_y("scalar", 7, 1)
         planes((6,))
@@ -383,10 +395,13 @@ def tile_metabolite_factor_diagnosis_weights_h2_kernel(
         store_codes((4, 5))
         for g in range(3):
             turn((7,), g)
-        finish((6,))
+        for g in range(3):
+            quantize_y((6,), g)
         gather_words("scalar", (7,), 0)
         gather_words("scalar", (7,), 1)
         gather_words("vector", (7,), 2)
-        finish((7,))
+        for g in range(3):
+            quantize_y((7,), g)
+        store_codes((6, 7))
         for q in range(4):
             store_scales(1, q, nc.scalar if q % 2 else nc.sync)

@@ -74,9 +74,9 @@ def tile_metabolite_factor_diagnosis_weights_h2_kernel(
             x_code.update({(h, k): t[:, k - k0, :] for k in range(k0, k1)})
 
         def load_l(k0, k1):
-            t = kept("l_raw%d" % k0, [P, k1 - k0, 512], I32)
-            nc.sync.dma_start(out=t[:], in_=l_words[k0:k1].rearrange("k p b -> p k b").bitcast(I32))
-            l_raw.update({(g, k): t[:, k - k0, g * 256 : (g + 1) * 256] for k in range(k0, k1) for g in range(2)})
+            t = kept("l_raw%d" % k0, [P, k1 - k0, 2048], U8)
+            nc.sync.dma_start(out=t[:].bitcast(I32), in_=l_words[k0:k1].rearrange("k p b -> p k b").bitcast(I32))
+            l_raw.update({(g, k): t[:, k - k0, g * 1024 : (g + 1) * 1024] for k in range(k0, k1) for g in range(2)})
 
         def load_scales(queue, plane, rows, half, quadrants=(0, 2, 1, 3)):
             for q in quadrants:
@@ -85,23 +85,22 @@ def tile_metabolite_factor_diagnosis_weights_h2_kernel(
 
         def load_a(g, c0, c1):
             t = kept("a_raw%d_%d" % (g, c0), [P, 4, (c1 - c0) * W], BF16)
-            rows = assoc[g * W : (g + 1) * W, c0 * W : c1 * W].rearrange("(q t r) n -> t q r n", t=4, r=8)
-            for slot in range(4):
-                nc.sync.dma_start(out=t[:, slot, :], in_=rows[slot])
+            rows = assoc[g * W : (g + 1) * W, c0 * W : c1 * W].rearrange("(p t) n -> p t n", t=4)
+            nc.sync.dma_start(out=t[:], in_=rows)
             a_raw.update({(g, c): t[:, :, (c - c0) * W : (c - c0 + 1) * W] for c in range(c0, c1)})
 
         def sort_l(g, k):
             t = kept("l_code%d_%d" % (g, k), [P, 1024], U8)
             nc.vector.tensor_copy(
-                out=t[:].bitcast(I32).rearrange("p (t q w) -> p t q w", t=4, w=4),
-                in_=l_raw[g, k].rearrange("p (q t w) -> p t q w", t=4, w=4),
+                out=t[:].rearrange("p (t q b) -> p t q b", t=4, b=2),
+                in_=l_raw[g, k].rearrange("p (q t b) -> p t q b", t=4, b=2),
             )
             l_code.update({(g, k): t})
 
-        def sort_l_scales(g):
+        def sort_l_scales(g, k0, k1):
             nc.vector.tensor_copy(
-                out=l_scale[g][:].bitcast(I32).rearrange("p k (t q w) -> p k t q w", t=4, w=2),
-                in_=l_scale_raw[g][:].bitcast(I32).rearrange("p k (q t w) -> p k t q w", t=4, w=2),
+                out=l_scale[g][:, k0:k1, :].rearrange("p k (t q) -> p k t q", t=4),
+                in_=l_scale_raw[g][:, k0:k1, :].rearrange("p k (q t) -> p k t q", t=4),
             )
 
         def interleave(engine, store, key, name, src, part, parts):
@@ -288,9 +287,9 @@ def tile_metabolite_factor_diagnosis_weights_h2_kernel(
         load_x(0, 1, 2)
         load_l(1, 2)
         load_scales(nc.sync, l_scale_raw[1], l_scales, 1)
-        load_a(0, 0, 1)
-        load_x(0, 2, 4)
         load_l(2, 4)
+        load_x(0, 2, 4)
+        load_a(0, 0, 1)
         load_a(1, 0, 2)
         load_scales(nc.sync, x_scale[1], x_scales, 1)
         load_x(1, 0, 2)
@@ -301,17 +300,21 @@ def tile_metabolite_factor_diagnosis_weights_h2_kernel(
         spread_bias()
         sort_l(0, 0)
         sort_l(1, 0)
-        sort_l_scales(0)
+        sort_l_scales(0, 0, 2)
+        sort_l_scales(0, 2, 4)
         sort_l(0, 1)
-        sort_l_scales(1)
+        sort_l_scales(1, 0, 2)
         sort_l(1, 1)
         for g, k in ((0, 0), (0, 1), (1, 0), (1, 1)):
             for slot in range(4):
                 factor_pass(0, g, slot, k)
-        interleave_a("vector", 0, 0)
-        for g in range(2):
-            sort_l(g, 2)
-            sort_l(g, 3)
+        sort_l(0, 2)
+        sort_l(0, 3)
+        sort_l_scales(1, 2, 4)
+        sort_l(1, 2)
+        sort_l(1, 3)
+        interleave_a("scalar", 0, 0, 0, 2)
+        interleave_a("vector", 0, 0, 1, 2)
         quantize_a(0, 0)
         for g in range(2):
             for slot in range(4):

from contextlib import ExitStack

import concourse.mybir as mybir
from concourse.masks import make_identity

M, K, F, N = 1024, 2048, 1024, 1536
FLOPS = 2 * M * K * F + 2 * M * F * N

F32 = mybir.dt.float32
BF16 = mybir.dt.bfloat16
I32 = mybir.dt.int32
U32 = mybir.dt.uint32
U8 = mybir.dt.uint8
FP8X4 = mybir.dt.float8_e4m3fn_x4
FP4X4 = mybir.dt.float4_e2m1fn_x4
ACT = mybir.ActivationFunctionType
ALU = mybir.AluOpType

P = 128
W = 512


def tile_metabolite_factor_diagnosis_weights_h2_kernel(
    tc, x_words, x_scales, l_words, l_scales, assoc, bias, out_0, out_1, out_2
):
    nc = tc.nc
    with ExitStack() as ctx:
        keep = ctx.enter_context(tc.tile_pool(name="keep", bufs=1))
        work = ctx.enter_context(tc.tile_pool(name="work", bufs=2))
        psum = ctx.enter_context(tc.psum_pool(name="psum", bufs=1))
        ctx.enter_context(tc.manual_schedule())

        banks_used = []

        def next_bank():
            index = len(banks_used) % 8
            bank = psum.tile([P, W], F32, name="bank%d" % index, tag="bank%d" % index)
            banks_used.append(bank)
            return bank

        def kept(name, shape, dtype):
            return keep.tile(shape, dtype, name=name, tag=name, align_bytes=256)

        x_code = {}
        x_scale = [kept("x_scale%d" % h, [P, 4, W], U8) for h in range(2)]
        l_raw = {}
        l_scale_raw = [kept("l_scale_raw%d" % g, [P, 4, W], U8) for g in range(2)]
        l_scale = [kept("l_scale%d" % g, [P, 4, W], U8) for g in range(2)]
        l_code = {}
        a_raw = {}
        a_code = [kept("a_code%d" % g, [P, N], U32) for g in range(2)]
        a_scale = [kept("a_scale%d" % g, [P, N], U8) for g in range(2)]
        a_words = {}
        h_bank = {}
        h_abs = {}
        h_words = {}
        h_code = {}
        h_scale = {}
        y_bank = {}
        y_f32 = {}
        y_bf = {}
        t_bank = {}
        yt_words = {}
        y_code = [kept("y_code%d" % h, [P, 3, W], U32) for h in range(2)]
        y_scale = [kept("y_scale%d" % h, [P, 3, W], U8) for h in range(2)]
        identity = kept("identity", [P, P], F32)
        bias_col = kept("bias_col", [P, 2, 6], BF16)
        bias_row = kept("bias_row", [P, N], BF16)

        def load_x(h, k0, k1):
            t = kept("x_code%d_%d" % (h, k0), [P, k1 - k0, W], U32)
            src = x_words[k0:k1].rearrange("k p m t -> p k (m t)")[:, :, h * 2048 : (h + 1) * 2048]
            nc.sync.dma_start(out=t[:].bitcast(I32), in_=src.bitcast(I32))
            x_code.update({(h, k): t[:, k - k0, :] for k in range(k0, k1)})

        def load_l(k0, k1):
            t = kept("l_raw%d" % k0, [P, k1 - k0, 2048], U8)
            nc.sync.dma_start(out=t[:].bitcast(I32), in_=l_words[k0:k1].rearrange("k p b -> p k b").bitcast(I32))
            l_raw.update({(g, k): t[:, k - k0, g * 1024 : (g + 1) * 1024] for k in range(k0, k1) for g in range(2)})

        def load_scales(queue, plane, rows, half, quadrants=(0, 2, 1, 3)):
            for q in quadrants:
                src = rows[:, 4 * q : 4 * q + 4, half * W : (half + 1) * W].rearrange("k r n -> r k n")
                queue.dma_start(out=plane[32 * q : 32 * q + 4, :, :].bitcast(I32), in_=src.bitcast(I32))

        def load_a(g, c0, c1):
            t = kept("a_raw%d_%d" % (g, c0), [P, 4, (c1 - c0) * W], BF16)
            rows = assoc[g * W : (g + 1) * W, c0 * W : c1 * W].rearrange("(p t) n -> p t n", t=4)
            nc.sync.dma_start(out=t[:], in_=rows)
            a_raw.update({(g, c): t[:, :, (c - c0) * W : (c - c0 + 1) * W] for c in range(c0, c1)})

        def sort_l(g, k):
            t = kept("l_code%d_%d" % (g, k), [P, 1024], U8)
            nc.vector.tensor_copy(
                out=t[:].rearrange("p (t q b) -> p t q b", t=4, b=2),
                in_=l_raw[g, k].rearrange("p (q t b) -> p t q b", t=4, b=2),
            )
            l_code.update({(g, k): t})

        def sort_l_scales(g, k0, k1):
            nc.vector.tensor_copy(
                out=l_scale[g][:, k0:k1, :].rearrange("p k (t q) -> p k t q", t=4),
                in_=l_scale_raw[g][:, k0:k1, :].rearrange("p k (q t) -> p k t q", t=4),
            )

        def interleave(engine, store, key, name, src, part, parts):
            if key not in store:
                store.update({key: work.tile([P, W, 4], BF16, name=name, tag=name, bufs=3, align_bytes=256)})
            cols = slice(part * W // parts, (part + 1) * W // parts)
            dst = store[key][:, cols, :].rearrange("p (c i) t -> p c t i", i=4)
            view = src[:, :, cols].rearrange("p t (c i) -> p c t i", i=4)
            if engine == "vector":
                nc.vector.tensor_copy(out=dst, in_=view)
            else:
                nc.scalar.copy(out=dst, in_=view)

        def interleave_a(engine, g, c, part=0, parts=1):
            interleave(engine, a_words, (g, c), "a_words", a_raw[g, c], part, parts)

        def quantize_a(g, c):
            cols = slice(c * W, (c + 1) * W)
            nc.vector.quantize_mx(
                out=a_code[g][:, cols].bitcast(FP8X4),
                scales=a_scale[g][:, cols],
                in_=a_words[g, c][:].rearrange("p n t -> p (n t)"),
            )

        def factor_pass(h, g, slot, k):
            if k == 0:
                h_bank.update({(h, g, slot): next_bank()})
            nc.tensor.matmul_mx(
                out=h_bank[h, g, slot][:],
                lhsT=l_code[g, k][:, slot * 256 : (slot + 1) * 256].bitcast(FP4X4),
                lhsT_scale=l_scale[g][:, k, slot * P : (slot + 1) * P],
                rhs=x_code[h, k].bitcast(FP8X4),
                rhs_scale=x_scale[h][:, k, :],
                start=(k == 0),
                stop=(k == 3),
            )

        def factor_slot(h, g, slot):
            for k in range(4):
                factor_pass(h, g, slot, k)

        def abs_slot(h, g, slot):
            if slot == 0:
                h_abs.update({(h, g): work.tile([P, 4, W], BF16, name="h_abs", tag="h_abs", align_bytes=256)})
            nc.scalar.activation(out=h_abs[h, g][:, slot, :], in_=h_bank[h, g, slot][:], func=ACT.Abs)

        def interleave_h(engine, h, g, part=0, parts=1):
            interleave(engine, h_words, (h, g), "h_words", h_abs[h, g][:], part, parts)

        def quantize_h(h, g):
            h_code.update({(h, g): kept("h_code%d_%d" % (h, g), [P, W], U32)})
            h_scale.update({(h, g): kept("h_scale%d_%d" % (h, g), [P, W], U8)})
            nc.vector.quantize_mx(
                out=h_code[h, g][:].bitcast(FP8X4),
                scales=h_scale[h, g][:],
                in_=h_words[h, g][:].rearrange("p m t -> p (m t)"),
            )

        def product(i, c):
            h, j = divmod(i, 4)
            rows = slice(j * P, (j + 1) * P)
            cols = slice(c * W, (c + 1) * W)
            bank = next_bank()
            y_bank.update({(i, c): bank})
            for g in range(2):
                nc.tensor.matmul_mx(
                    out=bank[:],
                    lhsT=h_code[h, g][:, rows].bitcast(FP8X4),
                    lhsT_scale=h_scale[h, g][:, rows],
                    rhs=a_code[g][:, cols].bitcast(FP8X4),
                    rhs_scale=a_scale[g][:, cols],
                    start=(g == 0),
                    stop=(g == 1),
                )

        def add_bias(i, c):
            if c == 0:
                y_f32.update({i: work.tile([P, N], F32, name="y_f32", tag="y_f32", bufs=6)})
            cols = slice(c * W, (c + 1) * W)
            nc.vector.tensor_tensor(out=y_f32[i][:, cols], in0=y_bank[i, c][:], in1=bias_row[:, cols], op=ALU.add)

        def round_y(engine, i, c):
            if i not in y_bf:
                y_bf.update({i: work.tile([P, N], BF16, name="y_bf", tag="y_bf", bufs=4, align_bytes=256)})
            cols = slice(c * W, (c + 1) * W)
            dst = y_bf[i][:, cols].rearrange("m (u p e) -> m u p e", u=2, e=2)
            src = y_f32[i][:, cols].rearrange("m (p u e) -> m u p e", u=2, e=2)
            if engine == "vector":
                nc.vector.tensor_copy(out=dst, in_=src)
            elif engine == "gpsimd":
                nc.gpsimd.tensor_scalar(out=dst, in0=src, scalar1=1.0, scalar2=0.0, op0=ALU.mult, op1=ALU.add)
            else:
                nc.scalar.copy(out=dst, in_=src)

        def store_y(i, c0=0, c1=3):
            nc.sync.dma_start(out=out_0[i * P : (i + 1) * P, c0 * W : c1 * W], in_=y_f32[i][:, c0 * W : c1 * W])

        def turn(tiles, g):
            bank = next_bank()
            t_bank.update({(tiles, g): bank})
            width = len(tiles) * P
            for j, i in enumerate(tiles):
                words = y_bf[i][:].bitcast(F32)
                for u in range(2):
                    nc.tensor.transpose(
                        bank[:, u * width + j * P : u * width + (j + 1) * P],
                        words[:, g * 256 + u * P : g * 256 + (u + 1) * P],
                        identity[:],
                    )

        def gather_words(engine, tiles, g):
            width = len(tiles) * P
            t = work.tile([P, 4 * width], BF16, name="yt_words", tag="yt_words", bufs=6, align_bytes=256)
            dst = t[:].bitcast(F32).rearrange("p (m u) -> p m u", u=2)
            src = t_bank[tiles, g][:, 0 : 2 * width].rearrange("p (u m) -> p m u", u=2)
            if engine == "vector":
                nc.vector.tensor_copy(out=dst, in_=src)
            else:
                nc.scalar.copy(out=dst, in_=src)
            yt_words.update({(tiles, g): t})

        def quantize_y(tiles, g):
            width = len(tiles) * P
            half, first = divmod(tiles[0] * P, W)
            nc.vector.quantize_mx(
                out=y_code[half][:, g, first : first + width].bitcast(FP8X4),
                scales=y_scale[half][:, g, first : first + width],
                in_=yt_words[tiles, g][:],
            )

        def store_codes(tiles, queue=nc.sync):
            dst = out_1.rearrange("g p m t -> p g (m t)")[:, :, tiles[0] * W : (tiles[-1] + 1) * W]
            half, first = divmod(tiles[0] * P, W)
            queue.dma_start(out=dst.bitcast(I32), in_=y_code[half][:, :, first : first + len(tiles) * P].bitcast(I32))

        def store_scales(half, q, queue=nc.sync):
            dst = out_2[:, 4 * q : 4 * q + 4, half * W : (half + 1) * W].rearrange("g r m -> r g m")
            queue.dma_start(out=dst.bitcast(I32), in_=y_scale[half][32 * q : 32 * q + 4, :, :].bitcast(I32))

        def spread_bias():
            for half in range(2):
                bank = next_bank()
                words = bias_col[:, half, :].bitcast(F32)
                for c in range(3):
                    nc.tensor.transpose(
                        bank[:, c * P : (c + 1) * P], words[:, c : c + 1].to_broadcast([P, P]), identity[:]
                    )
                nc.scalar.activation(
                    out=bias_row[:, half * 768 : (half + 1) * 768].rearrange("p (n c e) -> p n c e", c=3, e=2),
                    in_=bank[:, 0 : 3 * P].bitcast(BF16).rearrange("p (c n e) -> p n c e", c=3, e=2),
                    func=ACT.Copy,
                )


        def tile_product(i, gpsimd_rounds=(0, 1), by_chunk=False):
            for c in range(3):
                product(i, c)
                add_bias(i, c)
                if by_chunk:
                    store_y(i, c, c + 1)
                if c in gpsimd_rounds:
                    round_y("gpsimd", i, c)
            if not by_chunk:
                store_y(i)

        def planes(tiles):
            for g in range(3):
                turn(tiles, g)
                gather_words("scalar", tiles, g)

        def finish(tiles):
            for g in range(3):
                quantize_y(tiles, g)
            store_codes(tiles)

        nc.gpsimd.dma_start(out=bias_col[:], in_=bias.rearrange("(h p c) -> p h c", h=2, c=6))
        for plane in (l_scale_raw[0], x_scale[0], l_scale_raw[1], x_scale[1]):
            nc.vector.memset(plane[:].bitcast(I32), 0)
        make_identity(nc, identity[:])
        load_l(0, 1)
        load_x(0, 0, 1)
        load_scales(nc.sync, l_scale_raw[0], l_scales, 0)
        load_scales(nc.sync, x_scale[0], x_scales, 0)
        load_x(0, 1, 2)
        load_l(1, 2)
        load_scales(nc.sync, l_scale_raw[1], l_scales, 1)
        load_l(2, 4)
        load_x(0, 2, 4)
        load_a(0, 0, 1)
        load_a(1, 0, 2)
        load_scales(nc.sync, x_scale[1], x_scales, 1)
        load_x(1, 0, 2)
        load_x(1, 2, 4)
        load_a(0, 1, 3)
        load_a(1, 2, 3)

        spread_bias()
        sort_l(0, 0)
        sort_l(1, 0)
        sort_l_scales(0, 0, 2)
        sort_l_scales(0, 2, 4)
        sort_l(0, 1)
        sort_l_scales(1, 0, 2)
        sort_l(1, 1)
        for g, k in ((0, 0), (0, 1), (1, 0), (1, 1)):
            for slot in range(4):
                factor_pass(0, g, slot, k)
        sort_l(0, 2)
        sort_l(0, 3)
        sort_l_scales(1, 2, 4)
        sort_l(1, 2)
        sort_l(1, 3)
        interleave_a("scalar", 0, 0, 0, 2)
        interleave_a("vector", 0, 0, 1, 2)
        quantize_a(0, 0)
        for g in range(2):
            for slot in range(4):
                factor_pass(0, g, slot, 2)
                factor_pass(0, g, slot, 3)
                abs_slot(0, g, slot)
        interleave_a("vector", 1, 0)
        interleave_h("vector", 0, 0)
        quantize_a(1, 0)
        quantize_h(0, 0)
        interleave_a("scalar", 1, 1)
        interleave_h("vector", 0, 1)
        interleave_a("vector", 0, 1)
        quantize_h(0, 1)
        quantize_a(1, 1)
        quantize_a(0, 1)
        interleave_a("scalar", 0, 2)
        interleave_a("vector", 1, 2)
        for k in range(2):
            for slot in range(4):
                factor_pass(1, 0, slot, k)
        for slot in range(4):
            factor_pass(1, 0, slot, 2)
            factor_pass(1, 0, slot, 3)
            abs_slot(1, 0, slot)
        quantize_a(0, 2)
        quantize_a(1, 2)
        for slot in range(2):
            factor_slot(1, 1, slot)
            abs_slot(1, 1, slot)
        for c in range(2):
            product(0, c)
            add_bias(0, c)
        interleave_h("vector", 1, 0)
        for slot in range(2, 4):
            factor_slot(1, 1, slot)
            abs_slot(1, 1, slot)
            round_y("scalar", 0, slot - 2)
        product(0, 2)
        add_bias(0, 2)
        store_y(0)
        quantize_h(1, 0)
        interleave_h("scalar", 1, 1)
        round_y("gpsimd", 0, 2)
        tile_product(1, (0, 1))
        round_y("scalar", 1, 2)
        tile_product(2, (0,))
        quantize_h(1, 1)
        planes((0, 1))
        round_y("scalar", 2, 1)
        round_y("scalar", 2, 2)
        tile_product(3, (0,), True)
        round_y("scalar", 3, 1)
        round_y("scalar", 3, 2)
        finish((0, 1))
        tile_product(4, (0,), True)
        planes((2, 3))
        round_y("scalar", 4, 1)
        round_y("scalar", 4, 2)
        tile_product(5, (0,), True)
        round_y("scalar", 5, 1)
        round_y("scalar", 5, 2)
        finish((2, 3))
        for q in range(4):
            store_scales(0, q)
        tile_product(6)
        planes((4, 5))
        round_y("scalar", 6, 2)
        for c in range(3):
            product(7, c)
            add_bias(7, c)
            if c:
                store_y(7, 2 * c - 2, c + 1)
        round_y("gpsimd", 7, 0)
        round_y("scalar", 7, 1)
        planes((6,))
        quantize_y((4, 5), 0)
        round_y("vector", 7, 2)
        quantize_y((4, 5), 1)
        quantize_y((4, 5), 2)
        store_codes((4, 5))
        for g in range(3):
            turn((7,), g)
        for g in range(3):
            quantize_y((6,), g)
        gather_words("scalar", (7,), 0)
        gather_words("scalar", (7,), 1)
        gather_words("vector", (7,), 2)
        for g in range(3):
            quantize_y((7,), g)
        store_codes((6, 7))
        for q in range(4):
            store_scales(1, q, nc.scalar if q % 2 else nc.sync)
